import numpy as np
import ml_dtypes


def mxq(x, axis, fmt="e4m3"):
    dtype, down = {"e4m3": (ml_dtypes.float8_e4m3fn, 7), "e5m2": (ml_dtypes.float8_e5m2, 14)}[fmt]
    v = np.moveaxis(np.asarray(x, np.float32).astype(ml_dtypes.bfloat16).astype(np.float64), axis, -1)
    blocks = v.reshape(v.shape[:-1] + (-1, 32))
    amax = np.abs(blocks).max(-1, keepdims=True)
    byte = np.maximum(np.where(amax > 0, np.frexp(amax)[1] - 1 + 127, 0) - down, 1)
    scale = np.exp2(byte - 127.0)
    codes = (blocks / scale).astype(np.float32).astype(dtype).astype(np.float64)
    return np.moveaxis((codes * scale).reshape(v.shape), -1, axis)


WIDE = False


def mx_kscale(k):
    if not WIDE:
        return np.ones(k)
    levels = np.array([10, -10, 5, -5, 0])
    if k % 512:
        return np.exp2(np.random.permutation(np.resize(levels, k // 32))).repeat(32)
    a = np.empty((k // 512, 16))
    for p in range(k // 512):
        a[p, :8] = np.random.permutation(np.resize(levels, 8))
        for g in range(8):
            far = levels[np.abs(levels - a[p, g]) >= 10]
            a[p, g + 8] = far[np.random.randint(len(far))]
    return np.exp2(a.ravel()).repeat(32)


def f64(x):
    return np.asarray(x).astype(np.float64)


def striped(idx):
    return np.tile(idx.reshape(-1, 16).T, (8, 1)).astype(np.uint16)


def unstriped(offs):
    return offs[:16].T.reshape(-1).astype(np.int64)


def pack_weight(w):
    k, n = w.shape
    w = f64(np.asarray(w, np.float32).astype(ml_dtypes.bfloat16)).reshape(k // 32, 32, n)
    amax = np.abs(w).max(1)
    byte = np.clip(np.where(amax > 0, np.frexp(amax)[1] - 1 + 127 - 7, 1), 1, 254)
    scaled = (w * np.exp2(127.0 - byte)[:, None, :]).reshape(k, n).astype(np.float32)
    words = np.ascontiguousarray(scaled.reshape(k // 512, 128, 4, n).transpose(0, 1, 3, 2)).astype(ml_dtypes.float8_e4m3fn).view(np.uint8)
    return words, np.ascontiguousarray(byte.astype(np.uint8).reshape(k // 512, 16, n))


def unpack_weight(words, scales):
    g, p, n, _ = words.shape
    vals = np.ascontiguousarray(words).view(ml_dtypes.float8_e4m3fn).astype(np.float64) * np.repeat(np.exp2(scales.astype(np.float64) - 127.0), 8, axis=1)[..., None]
    return vals.transpose(0, 1, 3, 2).reshape(g * 512, n)


def sigmoid(v):
    return 1.0 / (1.0 + np.exp(-np.maximum(v, -700.0)))


K, T, S, D, N, H, V, U = 512, 2048, 1024, 4, 128, 512, 256, 512


def setup_inputs():
    n = np.random.standard_normal
    s = mx_kscale(K)[:, None]
    u = mx_kscale(H)
    packed_xT = pack_weight(n((K, T)) * s)
    return {
        "x_words": packed_xT[0],
        "x_scales": packed_xT[1],
        "w1": (n((K, H)) / np.sqrt(K) / s).astype(np.float32),
        "w2": (n((K, H)) / np.sqrt(K) / s).astype(np.float32),
        "fq": (np.random.uniform(0.4, 1.6, (H, U))).astype(np.float32),
        "unit": (np.random.uniform(0.6, 1.4, (H, 1)) * u[:, None]).astype(np.float32),
        "w3": (n((H, N)) / np.sqrt(H) / u[:, None]).astype(np.float32),
        "offs": striped(np.random.permutation(T)[:S]),
        "chd": striped(np.random.permutation(S)),
        "wl": striped(np.random.permutation(np.concatenate([np.arange(V), np.random.randint(0, V, U - V)]))),
    }


def reference(x_words, x_scales, w1, w2, fq, unit, w3, offs, chd, wl):
    xq = unpack_weight(x_words, x_scales)[:, unstriped(offs)]
    cs = mxq(f64(w1), 0, "e4m3").T @ xq
    cost = np.log(np.exp(cs) + 1.0)
    cc2_ = cost[:, unstriped(chd)]
    se = mxq(f64(w2), 0, "e4m3").T @ xq
    selv = sigmoid(se)
    inp = cc2_ * selv
    sc_ = selv[:, unstriped(chd)]
    nloop = inp * (sc_ + 0.3) + 0.4 * cost
    hash_ = inp + cost
    best = np.minimum(1.6 * nloop, hash_)
    plan = best.reshape(len(best), -1, D).sum(axis=2)
    tw = plan[:, unstriped(wl)]
    hid = f64(unit) * (np.log(tw + 0.2) * f64(fq))
    return mxq(f64(w3), 0, "e4m3").T @ mxq(hid, 0, "e4m3")

@@ -1,0 +1,285 @@
+from contextlib import ExitStack
+
+import concourse.mybir as mybir
+from concourse.masks import make_identity
+
+K, T, S, D, N, H, V, U = 512, 2048, 1024, 4, 128, 512, 256, 512
+FLOPS = 2 * K * H * S * 2 + 2 * H * N * U
+
+F32 = mybir.dt.float32
+BF16 = mybir.dt.bfloat16
+I32 = mybir.dt.int32
+U32 = mybir.dt.uint32
+U16 = mybir.dt.uint16
+U8 = mybir.dt.uint8
+FP8X4 = mybir.dt.float8_e4m3fn_x4
+ACT = mybir.ActivationFunctionType
+ALU = mybir.AluOpType
+
+P = 128
+PACK = 4
+HALF = 512
+TINY = 2.0 ** -40
+
+
+def tile_picked_ydbtune_log_p_kernel(
+    tc, x_words, x_scales, w1, w2, fq, unit, w3, offs, chd, wl, out
+):
+    nc = tc.nc
+    with ExitStack() as ctx:
+        keep = ctx.enter_context(tc.tile_pool(name="keep", bufs=1))
+        work = ctx.enter_context(tc.tile_pool(name="work", bufs=2))
+        psum = ctx.enter_context(tc.psum_pool(name="psum", bufs=1))
+
+        offs_sb = keep.tile([P, S // 16], U16, name="offs_sb")
+        chd_sb = keep.tile([P, S // 16], U16, name="chd_sb")
+        wl_sb = keep.tile([P, U // 16], U16, name="wl_sb")
+        x_table = keep.tile([P, T], I32, name="x_table")
+        x_scale_table = keep.tile([P, T], U8, name="x_scale_table")
+
+        x_scale_rows = keep.tile([P, T // 4], I32, name="x_scale_rows")
+        nc.vector.memset(x_scale_table[:].bitcast(I32), 0)
+        for quad in range(4):
+            nc.sync.dma_start(
+                x_scale_rows[32 * quad : 32 * quad + 4, :],
+                x_scales[0, 4 * quad : 4 * quad + 4, :].bitcast(I32),
+            )
+        nc.sync.dma_start(offs_sb[:], offs)
+        for quad in range(4):
+            rows = slice(32 * quad, 32 * quad + 4)
+            nc.vector.tensor_copy(x_scale_table[rows, :].bitcast(I32), x_scale_rows[rows, :])
+
+        def load_weight_half(w, h, name):
+            raw = keep.tile([P, PACK, H // 2], F32, name=name, tag=name)
+            nc.sync.dma_start(raw[:], w.rearrange("(p j) c -> p j c", j=PACK)[:, :, h * 256 : (h + 1) * 256])
+            return raw
+
+        w2_raw = [load_weight_half(w2, h, f"w2_raw{h}") for h in range(2)]
+        nc.sync.dma_start(x_table[:], x_words[0].rearrange("p n t -> p (n t)").bitcast(I32))
+        w1_raw = [load_weight_half(w1, h, f"w1_raw{h}") for h in range(2)]
+        nc.sync.dma_start(chd_sb[:], chd)
+        w3_raw = keep.tile([P, PACK, N], F32, name="w3_raw")
+        nc.sync.dma_start(w3_raw[:], w3.rearrange("(p j) c -> p j c", j=PACK))
+        unit_sb = keep.tile([P, PACK], F32, name="unit_sb")
+        nc.sync.dma_start(unit_sb[:], unit.rearrange("(p t) o -> p (t o)", t=PACK))
+        nc.sync.dma_start(wl_sb[:], wl)
+        fq_sb = keep.tile([P, PACK, U], F32, name="fq_sb")
+        nc.sync.dma_start(fq_sb[:], fq.rearrange("(p t) r -> p t r", t=PACK))
+
+        ident = keep.tile([P, P], F32, name="ident")
+        make_identity(nc, ident[:])
+
+        xg_words = [keep.tile([P, HALF], U32, name=f"xg_words{h}", align_bytes=64) for h in range(2)]
+        xg_scales = [keep.tile([P, HALF], U8, name=f"xg_scales{h}", align_bytes=64) for h in range(2)]
+        for h in range(2):
+            nc.vector.tensor_copy(xg_scales[h][:], x_scale_table[:].indirect(offs_sb[:, 32 * h : 32 * h + 32]))
+
+        def quantise_weight(raw, name, scalar_halves):
+            grouped = keep.tile([P, PACK, P, PACK], BF16, name=name + "_grouped", align_bytes=64)
+            codes = keep.tile([P, H], U32, name=name + "_codes", align_bytes=64)
+            scales = keep.tile([P, H], U8, name=name + "_scales", align_bytes=64)
+            for h in range(2):
+                dst = grouped[:, :, 64 * h : 64 * h + 64, :].rearrange("p t m j -> p m j t")
+                src = raw[h][:].rearrange("p j (m t) -> p m j t", t=PACK)
+                if h < scalar_halves:
+                    nc.scalar.copy(dst, src)
+                else:
+                    nc.vector.tensor_copy(dst, src)
+            flat = grouped[:].rearrange("p t m j -> p (t m j)")
+            for h in range(2):
+                nc.vector.quantize_mx(
+                    out=codes[:, 256 * h : 256 * h + 256].bitcast(FP8X4),
+                    scales=scales[:, 256 * h : 256 * h + 256],
+                    in_=flat[:, 1024 * h : 1024 * h + 1024],
+                )
+            return codes, scales
+
+        w2_mx = quantise_weight(w2_raw, "w2", 2)
+        for h in range(2):
+            nc.vector.tensor_copy(xg_words[h][:], x_table[:].bitcast(U32).indirect(offs_sb[:, 32 * h : 32 * h + 32]))
+        w1_mx = quantise_weight(w1_raw, "w1", 1)
+
+        w3_grouped = keep.tile([P, N, PACK], BF16, name="w3_grouped", align_bytes=64)
+        w3_codes = keep.tile([P, N], U32, name="w3_codes", align_bytes=64)
+        w3_scales = keep.tile([P, N], U8, name="w3_scales", align_bytes=64)
+        nc.vector.tensor_copy(w3_grouped[:], w3_raw[:].rearrange("p j c -> p c j"))
+        nc.vector.quantize_mx(
+            out=w3_codes[:].bitcast(FP8X4), scales=w3_scales[:], in_=w3_grouped[:].rearrange("p c j -> p (c j)")
+        )
+
+        def product(w_mx, t, h, tag, bufs):
+            bank = psum.tile([P, HALF], F32, name=f"{tag}{t}{h}", tag=tag, bufs=bufs)
+            codes, scales = w_mx
+            nc.tensor.matmul_mx(
+                out=bank[:],
+                lhsT=codes[:, P * t : P * (t + 1)].bitcast(FP8X4),
+                lhsT_scale=scales[:, P * t : P * (t + 1)],
+                rhs=xg_words[h][:].bitcast(FP8X4),
+                rhs_scale=xg_scales[h][:],
+                start=True,
+                stop=True,
+            )
+            return bank
+
+        cols = [slice(HALF * h, HALF * (h + 1)) for h in range(2)]
+        chd_half = [chd_sb[:, 32 * h : 32 * h + 32] for h in range(2)]
+        sig = [keep.tile([P, 2 * S], F32, name=f"sig{t}") for t in range(PACK)]
+        cs_banks = {}
+        logs = {}
+        cost = {}
+        factor = {}
+        planes = [keep.tile([P, V + 4 * P], F32, name=f"plane{t}") for t in range(PACK)]
+        hid = keep.tile([P, PACK, U], F32, name="hid")
+
+        def selectivity(t):
+            for h in range(2):
+                bank = product(w2_mx, t, h, "se", 2)
+                nc.scalar.activation(sig[t][:, cols[h]], bank[:], ACT.Sigmoid)
+
+        def cost_sigmoid(t):
+            for h in range(2):
+                cs_banks[t, h] = product(w1_mx, t, h, "cs", 4)
+                nc.scalar.activation(sig[t][:, S + HALF * h : S + HALF * (h + 1)], cs_banks[t, h][:], ACT.Sigmoid, scale=-1.0)
+
+        def cost_log(t):
+            logs[t] = work.tile([P, S], F32, name=f"logs{t}", tag="logs")
+            for h in range(2):
+                nc.scalar.activation(logs[t][:, cols[h]], sig[t][:, S + HALF * h : S + HALF * (h + 1)], ACT.Ln, bias=TINY)
+
+        def child_factor(t, h, on_vector):
+            factor[t, h] = work.tile([P, HALF], F32, name=f"factor{t}{h}", tag="factor", bufs=4)
+            picked = sig[t][:].indirect(chd_half[h])
+            if on_vector:
+                nc.vector.tensor_scalar(factor[t, h][:], picked, 1.6, -0.52, ALU.mult, ALU.add)
+            else:
+                nc.scalar.activation(factor[t, h][:], picked, ACT.Copy, bias=-0.52, scale=1.6)
+
+        def finish_cost(t):
+            cost[t] = work.tile([P, S], F32, name=f"cost{t}", tag="cost")
+            for h in range(2):
+                nc.vector.scalar_tensor_tensor(
+                    cost[t][:, cols[h]], logs[t][:, cols[h]], -1.0, cs_banks[t, h][:], ALU.mult, ALU.max
+                )
+
+        def add_transposed(dst, sources):
+            for n, src in enumerate(sources):
+                nc.tensor.matmul(dst, src, ident[:], start=(n == 0), stop=(n == len(sources) - 1), is_transpose=True)
+
+        def members(tile, h):
+            return [tile[:, HALF * h + d : HALF * (h + 1) : D] for d in range(D)]
+
+        def plan_sums(t):
+            cost_bank = psum.tile([P, V], F32, name=f"cost_bank{t}", tag="sum0")
+            for h in range(2):
+                add_transposed(cost_bank[:, P * h : P * (h + 1)], members(cost[t], h))
+            nc.scalar.activation(planes[t][:, V : 2 * V], cost_bank[:], ACT.Copy, scale=0.64)
+            inp = work.tile([P, S], F32, name=f"inp{t}", tag="inp")
+            for h in range(2):
+                nc.vector.tensor_tensor(inp[:, cols[h]], cost[t][:].indirect(chd_half[h]), sig[t][:, cols[h]], ALU.mult)
+            loop = work.tile([P, S], F32, name=f"loop{t}", tag="loop")
+            least = work.tile([P, 2, D, P], F32, name=f"least{t}", tag="least")
+            for h in range(2):
+                nc.vector.tensor_tensor(loop[:, cols[h]], inp[:, cols[h]], factor[t, h][:], ALU.mult)
+            for h in range(2):
+                nc.vector.scalar_tensor_tensor(
+                    least[:, h].rearrange("p d v -> p v d"),
+                    cost[t][:, cols[h]].rearrange("p (v d) -> p v d", d=D),
+                    0.36,
+                    loop[:, cols[h]].rearrange("p (v d) -> p v d", d=D),
+                    ALU.mult,
+                    ALU.min,
+                )
+            for h in range(2):
+                rest_bank = psum.tile([P, P], F32, name=f"rest_bank{t}{h}", tag=f"sum{h}")
+                add_transposed(rest_bank[:], members(inp, h) + [least[:, h, d, :] for d in range(D)])
+                nc.scalar.copy(planes[t][:, 2 * V + P * h : 2 * V + P * (h + 1)], rest_bank[:])
+
+        def plan_log(t):
+            plan_bank = psum.tile([P, HALF], F32, name=f"plan_bank{t}", tag="se", bufs=2)
+            for h in range(2):
+                add_transposed(
+                    plan_bank[:, P * h : P * (h + 1)],
+                    [planes[t][:, V + P * h : V + P * (h + 1)], planes[t][:, 2 * V + P * h : 2 * V + P * (h + 1)]],
+                )
+            nc.scalar.activation(planes[t][:, :V], plan_bank[:, :V], ACT.Ln, bias=0.2)
+
+        slot_logs = {}
+
+        def fetch_logs(t, pieces):
+            width = U // pieces
+            for n in range(pieces):
+                slot_logs[t, n] = work.tile([P, width], F32, name=f"slot_logs{t}{n}", tag="slot_logs", bufs=3)
+                nc.scalar.activation(
+                    slot_logs[t, n][:], planes[t][:].indirect(wl_sb[:, width // 16 * n : width // 16 * (n + 1)]), ACT.Copy
+                )
+
+        def hidden(t, pieces):
+            width = U // pieces
+            for n in range(pieces):
+                r = slice(width * n, width * (n + 1))
+                nc.vector.scalar_tensor_tensor(
+                    hid[:, t, r], slot_logs[t, n][:], unit_sb[:, t : t + 1], fq_sb[:, t, r], ALU.mult, ALU.mult
+                )
+
+        for t in (0, 1):
+            selectivity(t)
+        for t in (0, 1):
+            cost_sigmoid(t)
+        child_factor(0, 0, True)
+        child_factor(0, 1, True)
+        child_factor(1, 0, True)
+        for t in (0, 1):
+            cost_log(t)
+        finish_cost(0)
+        finish_cost(1)
+        for t in (2, 3):
+            selectivity(t)
+            cost_sigmoid(t)
+        child_factor(1, 1, False)
+        plan_sums(0)
+        for t in (2, 3):
+            cost_log(t)
+        plan_sums(1)
+        for t in (2, 3):
+            for h in range(2):
+                child_factor(t, h, False)
+        finish_cost(2)
+        finish_cost(3)
+        plan_log(0)
+        fetch_logs(0, 1)
+        plan_log(1)
+        fetch_logs(1, 1)
+        plan_sums(2)
+        plan_log(2)
+        fetch_logs(2, 1)
+        plan_sums(3)
+        hidden(0, 1)
+        hidden(1, 1)
+        hidden(2, 1)
+        plan_log(3)
+        fetch_logs(3, 2)
+        hidden(3, 2)
+
+        for h in range(2):
+            r = slice(256 * h, 256 * (h + 1))
+            grouped = work.tile([P, 256, PACK], BF16, name=f"hid_grouped{h}", tag="hid_grouped", align_bytes=64)
+            src = hid[:, :, r].rearrange("p t r -> p r t")
+            nc.vector.tensor_copy(grouped[:], src)
+            codes = work.tile([P, 256], U32, name=f"hid_codes{h}", tag="hid_codes", align_bytes=64)
+            scales = work.tile([P, 256], U8, name=f"hid_scales{h}", tag="hid_scales", align_bytes=64)
+            nc.vector.quantize_mx(
+                out=codes[:].bitcast(FP8X4), scales=scales[:], in_=grouped[:].rearrange("p r t -> p (r t)")
+            )
+            bank = psum.tile([P, HALF], F32, name=f"out_bank{h}", tag="cs", bufs=4)
+            nc.tensor.matmul_mx(
+                out=bank[:, :256],
+                lhsT=w3_codes[:].bitcast(FP8X4),
+                lhsT_scale=w3_scales[:],
+                rhs=codes[:].bitcast(FP8X4),
+                rhs_scale=scales[:],
+                start=True,
+                stop=True,
+            )
+            result = work.tile([P, 256], F32, name=f"result{h}", tag="result")
+            nc.scalar.copy(result[:], bank[:, :256])
+            nc.sync.dma_start(out[:, r], result[:])

@@ -37,67 +37,79 @@ def tile_picked_ydbtune_log_p_kernel(
         x_table = keep.tile([P, T], I32, name="x_table")
         x_scale_table = keep.tile([P, T], U8, name="x_scale_table")
 
-        x_scale_rows = keep.tile([P, T // 4], I32, name="x_scale_rows")
-        nc.vector.memset(x_scale_table[:].bitcast(I32), 0)
-        for quad in range(4):
-            nc.sync.dma_start(
-                x_scale_rows[32 * quad : 32 * quad + 4, :],
-                x_scales[0, 4 * quad : 4 * quad + 4, :].bitcast(I32),
-            )
-        nc.sync.dma_start(offs_sb[:], offs)
-        for quad in range(4):
-            rows = slice(32 * quad, 32 * quad + 4)
-            nc.vector.tensor_copy(x_scale_table[rows, :].bitcast(I32), x_scale_rows[rows, :])
-
-        def load_weight_half(w, h, name):
+        def load_weight_half(w, h, name, queue):
             raw = keep.tile([P, PACK, H // 2], F32, name=name, tag=name)
-            nc.sync.dma_start(raw[:], w.rearrange("(p j) c -> p j c", j=PACK)[:, :, h * 256 : (h + 1) * 256])
+            queue.dma_start(raw[:], w.rearrange("(p j) c -> p j c", j=PACK)[:, :, h * 256 : (h + 1) * 256])
             return raw
 
-        w2_raw = [load_weight_half(w2, h, f"w2_raw{h}") for h in range(2)]
-        nc.sync.dma_start(x_table[:], x_words[0].rearrange("p n t -> p (n t)").bitcast(I32))
-        w1_raw = [load_weight_half(w1, h, f"w1_raw{h}") for h in range(2)]
+        nc.vector.memset(x_scale_table[:].bitcast(I32), 0)
+        w1_raw = [load_weight_half(w1, 0, "w1_raw0", nc.scalar)]
+        nc.sync.dma_start(offs_sb[:], offs)
         nc.sync.dma_start(chd_sb[:], chd)
+        for quad in range(4):
+            nc.sync.dma_start(
+                x_scale_table[32 * quad : 32 * quad + 4, :].bitcast(I32),
+                x_scales[0, 4 * quad : 4 * quad + 4, :].bitcast(I32),
+            )
+        nc.sync.dma_start(x_table[:], x_words[0].rearrange("p n t -> p (n t)").bitcast(I32))
+        w1_raw.append(load_weight_half(w1, 1, "w1_raw1", nc.sync))
+        w2_raw = [load_weight_half(w2, h, f"w2_raw{h}", nc.sync) for h in range(2)]
         w3_raw = keep.tile([P, PACK, N], F32, name="w3_raw")
-        nc.sync.dma_start(w3_raw[:], w3.rearrange("(p j) c -> p j c", j=PACK))
         unit_sb = keep.tile([P, PACK], F32, name="unit_sb")
-        nc.sync.dma_start(unit_sb[:], unit.rearrange("(p t) o -> p (t o)", t=PACK))
-        nc.sync.dma_start(wl_sb[:], wl)
         fq_sb = keep.tile([P, PACK, U], F32, name="fq_sb")
+        nc.sync.dma_start(w3_raw[:], w3.rearrange("(p j) c -> p j c", j=PACK))
+        nc.sync.dma_start(unit_sb[:], unit.rearrange("(p t) o -> p (t o)", t=PACK))
         nc.sync.dma_start(fq_sb[:], fq.rearrange("(p t) r -> p t r", t=PACK))
+        nc.sync.dma_start(wl_sb[:], wl)
 
         ident = keep.tile([P, P], F32, name="ident")
         make_identity(nc, ident[:])
+        warm = keep.tile([P, 1], F32, name="warm")
+        nc.scalar.activation(warm[:], ident[:, 0:1], ACT.Sigmoid)
 
         xg_words = [keep.tile([P, HALF], U32, name=f"xg_words{h}", align_bytes=64) for h in range(2)]
         xg_scales = [keep.tile([P, HALF], U8, name=f"xg_scales{h}", align_bytes=64) for h in range(2)]
-        for h in range(2):
+
+        def pick_scales(h):
             nc.vector.tensor_copy(xg_scales[h][:], x_scale_table[:].indirect(offs_sb[:, 32 * h : 32 * h + 32]))
 
-        def quantise_weight(raw, name, scalar_halves):
+        def pick_words(h):
+            nc.vector.tensor_copy(xg_words[h][:], x_table[:].bitcast(U32).indirect(offs_sb[:, 32 * h : 32 * h + 32]))
+
+        def weight_tiles(name):
             grouped = keep.tile([P, PACK, P, PACK], BF16, name=name + "_grouped", align_bytes=64)
             codes = keep.tile([P, H], U32, name=name + "_codes", align_bytes=64)
             scales = keep.tile([P, H], U8, name=name + "_scales", align_bytes=64)
-            for h in range(2):
-                dst = grouped[:, :, 64 * h : 64 * h + 64, :].rearrange("p t m j -> p m j t")
-                src = raw[h][:].rearrange("p j (m t) -> p m j t", t=PACK)
-                if h < scalar_halves:
-                    nc.scalar.copy(dst, src)
-                else:
-                    nc.vector.tensor_copy(dst, src)
-            flat = grouped[:].rearrange("p t m j -> p (t m j)")
-            for h in range(2):
-                nc.vector.quantize_mx(
-                    out=codes[:, 256 * h : 256 * h + 256].bitcast(FP8X4),
-                    scales=scales[:, 256 * h : 256 * h + 256],
-                    in_=flat[:, 1024 * h : 1024 * h + 1024],
-                )
-            return codes, scales
+            return grouped, codes, scales
 
-        w2_mx = quantise_weight(w2_raw, "w2", 2)
-        for h in range(2):
-            nc.vector.tensor_copy(xg_words[h][:], x_table[:].bitcast(U32).indirect(offs_sb[:, 32 * h : 32 * h + 32]))
-        w1_mx = quantise_weight(w1_raw, "w1", 1)
+        def round_half(raw, tiles, h, copy):
+            copy(
+                tiles[0][:, :, 64 * h : 64 * h + 64, :].rearrange("p t m j -> p m j t"),
+                raw[h][:].rearrange("p j (m t) -> p m j t", t=PACK),
+            )
+
+        def quantise_tiles(tiles, first, count):
+            grouped, codes, scales = tiles
+            nc.vector.quantize_mx(
+                out=codes[:, P * first : P * (first + count)].bitcast(FP8X4),
+                scales=scales[:, P * first : P * (first + count)],
+                in_=grouped[:, first : first + count].rearrange("p t m j -> p (t m j)"),
+            )
+
+        w2_tiles = weight_tiles("w2")
+        w1_tiles = weight_tiles("w1")
+        w2_mx = w2_tiles[1:]
+        w1_mx = w1_tiles[1:]
+        pick_scales(0)
+        pick_scales(1)
+        pick_words(0)
+        round_half(w1_raw, w1_tiles, 0, nc.scalar.copy)
+        round_half(w1_raw, w1_tiles, 1, nc.scalar.copy)
+        quantise_tiles(w1_tiles, 0, 2)
+        pick_words(1)
+        round_half(w2_raw, w2_tiles, 0, nc.vector.tensor_copy)
+        round_half(w2_raw, w2_tiles, 1, nc.vector.tensor_copy)
+        quantise_tiles(w2_tiles, 0, 1)
 
         w3_grouped = keep.tile([P, N, PACK], BF16, name="w3_grouped", align_bytes=64)
         w3_codes = keep.tile([P, N], U32, name="w3_codes", align_bytes=64)
@@ -123,7 +135,7 @@ def tile_picked_ydbtune_log_p_kernel(
 
         cols = [slice(HALF * h, HALF * (h + 1)) for h in range(2)]
         chd_half = [chd_sb[:, 32 * h : 32 * h + 32] for h in range(2)]
-        sig = [keep.tile([P, 2 * S], F32, name=f"sig{t}") for t in range(PACK)]
+        sig = [keep.tile([P, 2 * S], F32, name=f"sig{t}", tag="w2_raw1" if t == 1 else f"sig{t}") for t in range(PACK)]
         cs_banks = {}
         logs = {}
         cost = {}
@@ -131,9 +143,9 @@ def tile_picked_ydbtune_log_p_kernel(
         planes = [keep.tile([P, V + 4 * P], F32, name=f"plane{t}") for t in range(PACK)]
         hid = keep.tile([P, PACK, U], F32, name="hid")
 
-        def selectivity(t):
+        def selectivity(t, tags=(("se", 2), ("se", 2))):
             for h in range(2):
-                bank = product(w2_mx, t, h, "se", 2)
+                bank = product(w2_mx, t, h, *tags[h])
                 nc.scalar.activation(sig[t][:, cols[h]], bank[:], ACT.Sigmoid)
 
         def cost_sigmoid(t):
@@ -168,34 +180,58 @@ def tile_picked_ydbtune_log_p_kernel(
         def members(tile, h):
             return [tile[:, HALF * h + d : HALF * (h + 1) : D] for d in range(D)]
 
-        def plan_sums(t):
-            cost_bank = psum.tile([P, V], F32, name=f"cost_bank{t}", tag="sum0")
+        def cost_sums(t, tag, bufs):
+            bank = psum.tile([P, V], F32, name=f"cost_bank{t}", tag=tag, bufs=bufs)
             for h in range(2):
-                add_transposed(cost_bank[:, P * h : P * (h + 1)], members(cost[t], h))
-            nc.scalar.activation(planes[t][:, V : 2 * V], cost_bank[:], ACT.Copy, scale=0.64)
-            inp = work.tile([P, S], F32, name=f"inp{t}", tag="inp")
+                add_transposed(bank[:, P * h : P * (h + 1)], members(cost[t], h))
+            nc.scalar.activation(planes[t][:, V : 2 * V], bank[:], ACT.Copy, scale=0.64)
+
+        inp = {}
+        loop = {}
+        least = {}
+
+        def inputs(t, h):
+            inp[t, h] = work.tile([P, HALF], F32, name=f"inp{t}{h}", tag="inp", bufs=4)
+            nc.vector.tensor_tensor(inp[t, h][:], cost[t][:].indirect(chd_half[h]), sig[t][:, cols[h]], ALU.mult)
+
+        def inputs_split(t, h):
+            child = work.tile([P, HALF], F32, name=f"child{t}{h}", tag="child")
+            nc.scalar.activation(child[:], cost[t][:].indirect(chd_half[h]), ACT.Copy)
+            inp[t, h] = work.tile([P, HALF], F32, name=f"inp{t}{h}", tag="inp", bufs=4)
+            nc.vector.tensor_tensor(inp[t, h][:], child[:], sig[t][:, cols[h]], ALU.mult)
+
+        def loops(t, h):
+            loop[t, h] = work.tile([P, HALF], F32, name=f"loop{t}{h}", tag="loop")
+            nc.vector.tensor_tensor(loop[t, h][:], inp[t, h][:], factor[t, h][:], ALU.mult)
+
+        def lesser(t, h):
+            least[t, h] = work.tile([P, D, P], F32, name=f"least{t}{h}", tag="least", bufs=4)
+            nc.vector.scalar_tensor_tensor(
+                least[t, h][:].rearrange("p d v -> p v d"),
+                cost[t][:, cols[h]].rearrange("p (v d) -> p v d", d=D),
+                0.36,
+                loop[t, h][:].rearrange("p (v d) -> p v d", d=D),
+                ALU.mult,
+                ALU.min,
+            )
+
+        def rest_sums(t, h, tag, bufs):
+            bank = psum.tile([P, P], F32, name=f"rest_bank{t}{h}", tag=tag, bufs=bufs)
+            add_transposed(bank[:], [inp[t, h][:, d::D] for d in range(D)] + [least[t, h][:, d, :] for d in range(D)])
+            nc.scalar.copy(planes[t][:, 2 * V + P * h : 2 * V + P * (h + 1)], bank[:])
+
+        def join_choice(t, tags, split=()):
             for h in range(2):
-                nc.vector.tensor_tensor(inp[:, cols[h]], cost[t][:].indirect(chd_half[h]), sig[t][:, cols[h]], ALU.mult)
-            loop = work.tile([P, S], F32, name=f"loop{t}", tag="loop")
-            least = work.tile([P, 2, D, P], F32, name=f"least{t}", tag="least")
+                (inputs_split if h in split else inputs)(t, h)
             for h in range(2):
-                nc.vector.tensor_tensor(loop[:, cols[h]], inp[:, cols[h]], factor[t, h][:], ALU.mult)
+                loops(t, h)
             for h in range(2):
-                nc.vector.scalar_tensor_tensor(
-                    least[:, h].rearrange("p d v -> p v d"),
-                    cost[t][:, cols[h]].rearrange("p (v d) -> p v d", d=D),
-                    0.36,
-                    loop[:, cols[h]].rearrange("p (v d) -> p v d", d=D),
-                    ALU.mult,
-                    ALU.min,
-                )
+                lesser(t, h)
             for h in range(2):
-                rest_bank = psum.tile([P, P], F32, name=f"rest_bank{t}{h}", tag=f"sum{h}")
-                add_transposed(rest_bank[:], members(inp, h) + [least[:, h, d, :] for d in range(D)])
-                nc.scalar.copy(planes[t][:, 2 * V + P * h : 2 * V + P * (h + 1)], rest_bank[:])
+                rest_sums(t, h, *tags[h])
 
         def plan_log(t):
-            plan_bank = psum.tile([P, HALF], F32, name=f"plan_bank{t}", tag="se", bufs=2)
+            plan_bank = psum.tile([P, HALF], F32, name=f"plan_bank{t}", tag="cs", bufs=4)
             for h in range(2):
                 add_transposed(
                     plan_bank[:, P * h : P * (h + 1)],
@@ -203,6 +239,21 @@ def tile_picked_ydbtune_log_p_kernel(
                 )
             nc.scalar.activation(planes[t][:, :V], plan_bank[:, :V], ACT.Ln, bias=0.2)
 
+        def weigh_frequencies(t):
+            nc.gpsimd.tensor_scalar(fq_unit[:, t, :], fq_sb[:, t, :], unit_sb[:, t : t + 1], 0.0, ALU.mult, ALU.add)
+
+        def hidden_fused(t, pieces):
+            width = U // pieces
+            for n in range(pieces):
+                r = slice(width * n, width * (n + 1))
+                nc.vector.tensor_tensor(
+                    hid[:, t, r],
+                    planes[t][:].indirect(wl_sb[:, width // 16 * n : width // 16 * (n + 1)]),
+                    fq_unit[:, t, r],
+                    ALU.mult,
+                )
+
+        fq_unit = keep.tile([P, PACK, U], F32, name="fq_unit")
         slot_logs = {}
 
         def fetch_logs(t, pieces):
@@ -221,58 +272,76 @@ def tile_picked_ydbtune_log_p_kernel(
                     hid[:, t, r], slot_logs[t, n][:], unit_sb[:, t : t + 1], fq_sb[:, t, r], ALU.mult, ALU.mult
                 )
 
-        for t in (0, 1):
-            selectivity(t)
-        for t in (0, 1):
-            cost_sigmoid(t)
+        cost_sigmoid(0)
+        cost_sigmoid(1)
+        selectivity(0)
+        quantise_tiles(w2_tiles, 1, 1)
+        quantise_tiles(w2_tiles, 2, 2)
+        quantise_tiles(w1_tiles, 2, 2)
+        for t in (2, 3):
+            weigh_frequencies(t)
         child_factor(0, 0, True)
         child_factor(0, 1, True)
-        child_factor(1, 0, True)
         for t in (0, 1):
             cost_log(t)
         finish_cost(0)
         finish_cost(1)
-        for t in (2, 3):
-            selectivity(t)
-            cost_sigmoid(t)
+        selectivity(1, (("sum0", 1), ("sum1", 1)))
+        selectivity(2)
+        selectivity(3, (("sum0", 1), ("sum1", 1)))
+        cost_sigmoid(2)
+        cost_sigmoid(3)
         child_factor(1, 1, False)
-        plan_sums(0)
-        for t in (2, 3):
-            cost_log(t)
-        plan_sums(1)
-        for t in (2, 3):
-            for h in range(2):
-                child_factor(t, h, False)
+        cost_sums(0, "se", 2)
+        cost_sums(1, "se", 2)
+        cost_log(2)
+        join_choice(0, [("sum0", 1), ("sum1", 1)])
+        cost_log(3)
+        child_factor(1, 0, True)
+        join_choice(1, [("se", 2), ("se", 2)])
         finish_cost(2)
         finish_cost(3)
+        child_factor(2, 0, False)
+        child_factor(2, 1, False)
+        cost_sums(2, "sum0", 1)
+        cost_sums(3, "sum1", 1)
         plan_log(0)
-        fetch_logs(0, 1)
+        child_factor(3, 0, False)
+        child_factor(3, 1, False)
         plan_log(1)
+        join_choice(2, [("se", 2), ("se", 2)])
+        fetch_logs(0, 1)
         fetch_logs(1, 1)
-        plan_sums(2)
         plan_log(2)
-        fetch_logs(2, 1)
-        plan_sums(3)
+        join_choice(3, [("sum0", 1), ("sum1", 1)])
+        plan_log(3)
         hidden(0, 1)
         hidden(1, 1)
-        hidden(2, 1)
-        plan_log(3)
-        fetch_logs(3, 2)
-        hidden(3, 2)
+        hidden_fused(2, 1)
 
-        for h in range(2):
-            r = slice(256 * h, 256 * (h + 1))
-            grouped = work.tile([P, 256, PACK], BF16, name=f"hid_grouped{h}", tag="hid_grouped", align_bytes=64)
-            src = hid[:, :, r].rearrange("p t r -> p r t")
-            nc.vector.tensor_copy(grouped[:], src)
-            codes = work.tile([P, 256], U32, name=f"hid_codes{h}", tag="hid_codes", align_bytes=64)
-            scales = work.tile([P, 256], U8, name=f"hid_scales{h}", tag="hid_scales", align_bytes=64)
-            nc.vector.quantize_mx(
-                out=codes[:].bitcast(FP8X4), scales=scales[:], in_=grouped[:].rearrange("p r t -> p (r t)")
+        pieces = [(0, 256, nc.scalar.copy), (256, 256, nc.vector.tensor_copy)]
+        last = PACK - 1
+        for first, width, copy in pieces:
+            r = slice(first, first + width)
+            nc.vector.tensor_tensor(
+                hid[:, last, r],
+                planes[last][:].indirect(wl_sb[:, first // 16 : (first + width) // 16]),
+                fq_unit[:, last, r],
+                ALU.mult,
             )
-            bank = psum.tile([P, HALF], F32, name=f"out_bank{h}", tag="cs", bufs=4)
+        grouped = {}
+        for first, width, copy in pieces:
+            grouped[first] = keep.tile([P, width, PACK], BF16, name=f"hid_grouped{first}", align_bytes=64)
+            copy(grouped[first][:], hid[:, :, first : first + width].rearrange("p t r -> p r t"))
+        for first, width, copy in pieces:
+            codes = keep.tile([P, width], U32, name=f"hid_codes{first}", align_bytes=64)
+            scales = keep.tile([P, width], U8, name=f"hid_scales{first}", align_bytes=64)
+            nc.vector.quantize_mx(
+                out=codes[:].bitcast(FP8X4), scales=scales[:], in_=grouped[first][:].rearrange("p r t -> p (r t)")
+            )
+            bank = psum.tile([P, width], F32, name=f"out_bank{first}", tag="cs", bufs=4)
             nc.tensor.matmul_mx(
-                out=bank[:, :256],
+                out=bank[:],
                 lhsT=w3_codes[:].bitcast(FP8X4),
                 lhsT_scale=w3_scales[:],
                 rhs=codes[:].bitcast(FP8X4),
@@ -280,6 +349,6 @@ def tile_picked_ydbtune_log_p_kernel(
                 start=True,
                 stop=True,
             )
-            result = work.tile([P, 256], F32, name=f"result{h}", tag="result")
-            nc.scalar.copy(result[:], bank[:, :256])
-            nc.sync.dma_start(out[:, r], result[:])
+            result = keep.tile([P, width], F32, name=f"result{first}")
+            nc.scalar.copy(result[:], bank[:])
+            nc.sync.dma_start(out[:, first : first + width], result[:])

@@ -82,10 +82,10 @@ def tile_picked_ydbtune_log_p_kernel(
             scales = keep.tile([P, H], U8, name=name + "_scales", align_bytes=64)
             return grouped, codes, scales
 
-        def round_half(raw, tiles, h, copy):
+        def round_half(raw, tiles, h, copy, first=0, count=PACK):
             copy(
-                tiles[0][:, :, 64 * h : 64 * h + 64, :].rearrange("p t m j -> p m j t"),
-                raw[h][:].rearrange("p j (m t) -> p m j t", t=PACK),
+                tiles[0][:, first : first + count, 64 * h : 64 * h + 64, :].rearrange("p t m j -> p m j t"),
+                raw[h][:].rearrange("p j (m t) -> p m j t", t=PACK)[:, :, :, first : first + count],
             )
 
         def quantise_tiles(tiles, first, count):
@@ -104,11 +104,12 @@ def tile_picked_ydbtune_log_p_kernel(
         pick_scales(1)
         pick_words(0)
         round_half(w1_raw, w1_tiles, 0, nc.scalar.copy)
-        round_half(w1_raw, w1_tiles, 1, nc.scalar.copy)
+        round_half(w1_raw, w1_tiles, 1, nc.scalar.copy, 0, 2)
         quantise_tiles(w1_tiles, 0, 2)
         pick_words(1)
-        round_half(w2_raw, w2_tiles, 0, nc.vector.tensor_copy)
-        round_half(w2_raw, w2_tiles, 1, nc.vector.tensor_copy)
+        round_half(w1_raw, w1_tiles, 1, nc.scalar.copy, 2, 2)
+        round_half(w2_raw, w2_tiles, 0, nc.vector.tensor_copy, 0, 2)
+        round_half(w2_raw, w2_tiles, 1, nc.vector.tensor_copy, 0, 2)
         quantise_tiles(w2_tiles, 0, 1)
 
         w3_grouped = keep.tile([P, N, PACK], BF16, name="w3_grouped", align_bytes=64)
@@ -135,7 +136,7 @@ def tile_picked_ydbtune_log_p_kernel(
 
         cols = [slice(HALF * h, HALF * (h + 1)) for h in range(2)]
         chd_half = [chd_sb[:, 32 * h : 32 * h + 32] for h in range(2)]
-        sig = [keep.tile([P, 2 * S], F32, name=f"sig{t}", tag="w2_raw1" if t == 1 else f"sig{t}") for t in range(PACK)]
+        sig = [keep.tile([P, 2 * S], F32, name=f"sig{t}") for t in range(PACK)]
         cs_banks = {}
         logs = {}
         cost = {}
@@ -154,7 +155,10 @@ def tile_picked_ydbtune_log_p_kernel(
                 nc.scalar.activation(sig[t][:, S + HALF * h : S + HALF * (h + 1)], cs_banks[t, h][:], ACT.Sigmoid, scale=-1.0)
 
         def cost_log(t):
-            logs[t] = work.tile([P, S], F32, name=f"logs{t}", tag="logs")
+            if t % 2 == 0:
+                tag = "w2_grouped" if t == 0 else "w1_grouped"
+                logs["pair"] = keep.tile([P, 2, S], F32, name=f"logs{t}", tag=tag, align_bytes=64)
+            logs[t] = logs["pair"][:, t % 2, :]
             for h in range(2):
                 nc.scalar.activation(logs[t][:, cols[h]], sig[t][:, S + HALF * h : S + HALF * (h + 1)], ACT.Ln, bias=TINY)
 
@@ -205,19 +209,19 @@ def tile_picked_ydbtune_log_p_kernel(
             nc.vector.tensor_tensor(loop[t, h][:], inp[t, h][:], factor[t, h][:], ALU.mult)
 
         def lesser(t, h):
-            least[t, h] = work.tile([P, D, P], F32, name=f"least{t}{h}", tag="least", bufs=4)
+            least[t, h] = work.tile([P, 2, 2 * P], F32, name=f"least{t}{h}", tag="least", bufs=4)
             nc.vector.scalar_tensor_tensor(
-                least[t, h][:].rearrange("p d v -> p v d"),
-                cost[t][:, cols[h]].rearrange("p (v d) -> p v d", d=D),
+                least[t, h][:].rearrange("p e w -> p w e"),
+                cost[t][:, cols[h]].rearrange("p (w e) -> p w e", e=2),
                 0.36,
-                loop[t, h][:].rearrange("p (v d) -> p v d", d=D),
+                loop[t, h][:].rearrange("p (w e) -> p w e", e=2),
                 ALU.mult,
                 ALU.min,
             )
 
         def rest_sums(t, h, tag, bufs):
             bank = psum.tile([P, P], F32, name=f"rest_bank{t}{h}", tag=tag, bufs=bufs)
-            add_transposed(bank[:], [inp[t, h][:, d::D] for d in range(D)] + [least[t, h][:, d, :] for d in range(D)])
+            add_transposed(bank[:], [inp[t, h][:, d::D] for d in range(D)] + [least[t, h][:, d % 2, d // 2 :: 2] for d in range(D)])
             nc.scalar.copy(planes[t][:, 2 * V + P * h : 2 * V + P * (h + 1)], bank[:])
 
         def join_choice(t, tags, split=()):
@@ -276,9 +280,11 @@ def tile_picked_ydbtune_log_p_kernel(
         cost_sigmoid(1)
         selectivity(0)
         quantise_tiles(w2_tiles, 1, 1)
+        round_half(w2_raw, w2_tiles, 0, nc.vector.tensor_copy, 2, 2)
+        round_half(w2_raw, w2_tiles, 1, nc.vector.tensor_copy, 2, 2)
         quantise_tiles(w2_tiles, 2, 2)
         quantise_tiles(w1_tiles, 2, 2)
-        for t in (2, 3):
+        for t in (3,):
             weigh_frequencies(t)
         child_factor(0, 0, True)
         child_factor(0, 1, True)
@@ -287,13 +293,13 @@ def tile_picked_ydbtune_log_p_kernel(
         finish_cost(0)
         finish_cost(1)
         selectivity(1, (("sum0", 1), ("sum1", 1)))
-        selectivity(2)
-        selectivity(3, (("sum0", 1), ("sum1", 1)))
         cost_sigmoid(2)
         cost_sigmoid(3)
-        child_factor(1, 1, False)
         cost_sums(0, "se", 2)
         cost_sums(1, "se", 2)
+        selectivity(2, (("sum0", 1), ("sum1", 1)))
+        selectivity(3)
+        child_factor(1, 1, False)
         cost_log(2)
         join_choice(0, [("sum0", 1), ("sum1", 1)])
         cost_log(3)
@@ -313,13 +319,14 @@ def tile_picked_ydbtune_log_p_kernel(
         fetch_logs(0, 1)
         fetch_logs(1, 1)
         plan_log(2)
+        fetch_logs(2, 1)
         join_choice(3, [("sum0", 1), ("sum1", 1)])
         plan_log(3)
         hidden(0, 1)
         hidden(1, 1)
-        hidden_fused(2, 1)
+        hidden(2, 1)
 
-        pieces = [(0, 256, nc.scalar.copy), (256, 256, nc.vector.tensor_copy)]
+        pieces = [(0, 128, nc.scalar.copy), (128, 128, nc.vector.tensor_copy), (256, 128, nc.scalar.copy), (384, 128, nc.vector.tensor_copy)]
         last = PACK - 1
         for first, width, copy in pieces:
             r = slice(first, first + width)

@@ -19,7 +19,9 @@ ALU = mybir.AluOpType
 P = 128
 PACK = 4
 HALF = 512
+QUARTER = 128
 TINY = 2.0 ** -40
+COST_SHARE = 0.64
 
 
 def tile_picked_ydbtune_log_p_kernel(
@@ -36,14 +38,15 @@ def tile_picked_ydbtune_log_p_kernel(
         wl_sb = keep.tile([P, U // 16], U16, name="wl_sb")
         x_table = keep.tile([P, T], I32, name="x_table")
         x_scale_table = keep.tile([P, T], U8, name="x_scale_table")
+        sel = [keep.tile([P, 2 * S], F32, name=f"sel{t}") for t in range(PACK)]
 
-        def load_weight_half(w, h, name, queue):
-            raw = keep.tile([P, PACK, H // 2], F32, name=name, tag=name)
-            queue.dma_start(raw[:], w.rearrange("(p j) c -> p j c", j=PACK)[:, :, h * 256 : (h + 1) * 256])
+        def load_weight_half(w, h, tile, queue):
+            raw = tile[:, S:].rearrange("p (j c) -> p j c", j=PACK)
+            queue.dma_start(raw, w.rearrange("(p j) c -> p j c", j=PACK)[:, :, h * 256 : (h + 1) * 256])
             return raw
 
         nc.vector.memset(x_scale_table[:].bitcast(I32), 0)
-        w1_raw = [load_weight_half(w1, 0, "w1_raw0", nc.scalar)]
+        w2_raw = [load_weight_half(w2, 0, sel[0], nc.scalar)]
         nc.sync.dma_start(offs_sb[:], offs)
         nc.sync.dma_start(chd_sb[:], chd)
         for quad in range(4):
@@ -52,8 +55,8 @@ def tile_picked_ydbtune_log_p_kernel(
                 x_scales[0, 4 * quad : 4 * quad + 4, :].bitcast(I32),
             )
         nc.sync.dma_start(x_table[:], x_words[0].rearrange("p n t -> p (n t)").bitcast(I32))
-        w1_raw.append(load_weight_half(w1, 1, "w1_raw1", nc.sync))
-        w2_raw = [load_weight_half(w2, h, f"w2_raw{h}", nc.sync) for h in range(2)]
+        w2_raw.append(load_weight_half(w2, 1, sel[1], nc.sync))
+        w1_raw = [load_weight_half(w1, h, sel[2 + h], nc.sync) for h in range(2)]
         w3_raw = keep.tile([P, PACK, N], F32, name="w3_raw")
         unit_sb = keep.tile([P, PACK], F32, name="unit_sb")
         fq_sb = keep.tile([P, PACK, U], F32, name="fq_sb")
@@ -69,12 +72,9 @@ def tile_picked_ydbtune_log_p_kernel(
 
         xg_words = [keep.tile([P, HALF], U32, name=f"xg_words{h}", align_bytes=64) for h in range(2)]
         xg_scales = [keep.tile([P, HALF], U8, name=f"xg_scales{h}", align_bytes=64) for h in range(2)]
-
-        def pick_scales(h):
-            nc.vector.tensor_copy(xg_scales[h][:], x_scale_table[:].indirect(offs_sb[:, 32 * h : 32 * h + 32]))
-
-        def pick_words(h):
-            nc.vector.tensor_copy(xg_words[h][:], x_table[:].bitcast(U32).indirect(offs_sb[:, 32 * h : 32 * h + 32]))
+        offs_half = [offs_sb[:, 32 * h : 32 * h + 32] for h in range(2)]
+        chd_half = [chd_sb[:, 32 * h : 32 * h + 32] for h in range(2)]
+        cols = [slice(HALF * h, HALF * (h + 1)) for h in range(2)]
 
         def weight_tiles(name):
             grouped = keep.tile([P, PACK, P, PACK], BF16, name=name + "_grouped", align_bytes=64)
@@ -82,13 +82,13 @@ def tile_picked_ydbtune_log_p_kernel(
             scales = keep.tile([P, H], U8, name=name + "_scales", align_bytes=64)
             return grouped, codes, scales
 
-        def round_half(raw, tiles, h, copy, first=0, count=PACK):
+        def round_part(raw, tiles, h, copy, first, count):
             copy(
                 tiles[0][:, first : first + count, 64 * h : 64 * h + 64, :].rearrange("p t m j -> p m j t"),
-                raw[h][:].rearrange("p j (m t) -> p m j t", t=PACK)[:, :, :, first : first + count],
+                raw[h].rearrange("p j (m t) -> p m j t", t=PACK)[:, :, :, first : first + count],
             )
 
-        def quantise_tiles(tiles, first, count):
+        def quantise_part(tiles, first, count):
             grouped, codes, scales = tiles
             nc.vector.quantize_mx(
                 out=codes[:, P * first : P * (first + count)].bitcast(FP8X4),
@@ -98,19 +98,19 @@ def tile_picked_ydbtune_log_p_kernel(
 
         w2_tiles = weight_tiles("w2")
         w1_tiles = weight_tiles("w1")
-        w2_mx = w2_tiles[1:]
-        w1_mx = w1_tiles[1:]
-        pick_scales(0)
-        pick_scales(1)
-        pick_words(0)
-        round_half(w1_raw, w1_tiles, 0, nc.scalar.copy)
-        round_half(w1_raw, w1_tiles, 1, nc.scalar.copy, 0, 2)
-        quantise_tiles(w1_tiles, 0, 2)
-        pick_words(1)
-        round_half(w1_raw, w1_tiles, 1, nc.scalar.copy, 2, 2)
-        round_half(w2_raw, w2_tiles, 0, nc.vector.tensor_copy, 0, 2)
-        round_half(w2_raw, w2_tiles, 1, nc.vector.tensor_copy, 0, 2)
-        quantise_tiles(w2_tiles, 0, 1)
+        for h in range(2):
+            nc.vector.tensor_copy(xg_scales[h][:], x_scale_table[:].indirect(offs_half[h]))
+        for h in range(2):
+            nc.vector.tensor_copy(xg_words[h][:], x_table[:].bitcast(U32).indirect(offs_half[h]))
+        round_part(w2_raw, w2_tiles, 0, nc.scalar.copy, 0, 4)
+        round_part(w2_raw, w2_tiles, 1, nc.scalar.copy, 0, 2)
+        quantise_part(w2_tiles, 0, 2)
+        round_part(w2_raw, w2_tiles, 1, nc.scalar.copy, 2, 2)
+        quantise_part(w2_tiles, 2, 2)
+        round_part(w1_raw, w1_tiles, 0, nc.vector.tensor_copy, 0, 4)
+        round_part(w1_raw, w1_tiles, 1, nc.vector.tensor_copy, 0, 4)
+        quantise_part(w1_tiles, 0, 2)
+        quantise_part(w1_tiles, 2, 2)
 
         w3_grouped = keep.tile([P, N, PACK], BF16, name="w3_grouped", align_bytes=64)
         w3_codes = keep.tile([P, N], U32, name="w3_codes", align_bytes=64)
@@ -120,235 +120,193 @@ def tile_picked_ydbtune_log_p_kernel(
             out=w3_codes[:].bitcast(FP8X4), scales=w3_scales[:], in_=w3_grouped[:].rearrange("p c j -> p (c j)")
         )
 
-        def product(w_mx, t, h, tag, bufs):
-            bank = psum.tile([P, HALF], F32, name=f"{tag}{t}{h}", tag=tag, bufs=bufs)
-            codes, scales = w_mx
+        def bank_tile(bank, width, name):
+            return psum.tile([P, width], F32, name=name, tag=f"bank{bank}")
+
+        def product(tiles, t, h, bank, name):
+            acc = bank_tile(bank, HALF, f"{name}{t}{h}")
             nc.tensor.matmul_mx(
-                out=bank[:],
-                lhsT=codes[:, P * t : P * (t + 1)].bitcast(FP8X4),
-                lhsT_scale=scales[:, P * t : P * (t + 1)],
+                out=acc[:],
+                lhsT=tiles[1][:, P * t : P * (t + 1)].bitcast(FP8X4),
+                lhsT_scale=tiles[2][:, P * t : P * (t + 1)],
                 rhs=xg_words[h][:].bitcast(FP8X4),
                 rhs_scale=xg_scales[h][:],
                 start=True,
                 stop=True,
             )
-            return bank
+            return acc
 
-        cols = [slice(HALF * h, HALF * (h + 1)) for h in range(2)]
-        chd_half = [chd_sb[:, 32 * h : 32 * h + 32] for h in range(2)]
-        sig = [keep.tile([P, 2 * S], F32, name=f"sig{t}") for t in range(PACK)]
-        cs_banks = {}
+        def cost_bank(t, h):
+            return (4 + 2 * t + h) % 8
+
+        cs = {}
+        cost_window = {}
+        miss = {}
         logs = {}
         cost = {}
         factor = {}
-        planes = [keep.tile([P, V + 4 * P], F32, name=f"plane{t}") for t in range(PACK)]
+        child = {}
+        inp = {}
+        loop = {}
+        least = {}
+        slot_logs = {}
+        planes = [keep.tile([P, 2 * V], F32, name=f"plane{t}") for t in range(PACK)]
         hid = keep.tile([P, PACK, U], F32, name="hid")
+        fq_unit2 = keep.tile([P, V], F32, name="fq_unit2")
+        fq_unit = keep.tile([P, V], F32, name="fq_unit")
 
-        def selectivity(t, tags=(("se", 2), ("se", 2))):
+        def selectivity(t):
             for h in range(2):
-                bank = product(w2_mx, t, h, *tags[h])
-                nc.scalar.activation(sig[t][:, cols[h]], bank[:], ACT.Sigmoid)
+                acc = product(w2_tiles, t, h, (2 * t + h) % 4, "se")
+                nc.scalar.activation(sel[t][:, cols[h]], acc[:], ACT.Sigmoid)
 
         def cost_sigmoid(t):
+            cost_window[t] = keep.tile([P, 2 * S], F32, name=f"cost{t}")
+            cost[t] = cost_window[t][:, :S]
+            miss[t] = cost_window[t][:, S:]
             for h in range(2):
-                cs_banks[t, h] = product(w1_mx, t, h, "cs", 4)
-                nc.scalar.activation(sig[t][:, S + HALF * h : S + HALF * (h + 1)], cs_banks[t, h][:], ACT.Sigmoid, scale=-1.0)
+                cs[t, h] = product(w1_tiles, t, h, cost_bank(t, h), "cs")
+                nc.scalar.activation(miss[t][:, cols[h]], cs[t, h][:], ACT.Sigmoid, scale=-1.0)
 
         def cost_log(t):
-            if t % 2 == 0:
-                tag = "w2_grouped" if t == 0 else "w1_grouped"
-                logs["pair"] = keep.tile([P, 2, S], F32, name=f"logs{t}", tag=tag, align_bytes=64)
-            logs[t] = logs["pair"][:, t % 2, :]
+            logs[t] = work.tile([P, S], F32, name=f"logs{t}", tag="logs")
             for h in range(2):
-                nc.scalar.activation(logs[t][:, cols[h]], sig[t][:, S + HALF * h : S + HALF * (h + 1)], ACT.Ln, bias=TINY)
+                nc.scalar.activation(logs[t][:, cols[h]], miss[t][:, cols[h]], ACT.Ln, bias=TINY)
 
-        def child_factor(t, h, on_vector):
-            factor[t, h] = work.tile([P, HALF], F32, name=f"factor{t}{h}", tag="factor", bufs=4)
-            picked = sig[t][:].indirect(chd_half[h])
+        def child_factor(t, h, on_vector=True):
+            factor[t, h] = keep.tile([P, HALF], F32, name=f"factor{t}{h}")
+            picked = sel[t][:].indirect(chd_half[h])
             if on_vector:
                 nc.vector.tensor_scalar(factor[t, h][:], picked, 1.6, -0.52, ALU.mult, ALU.add)
             else:
                 nc.scalar.activation(factor[t, h][:], picked, ACT.Copy, bias=-0.52, scale=1.6)
 
         def finish_cost(t):
-            cost[t] = work.tile([P, S], F32, name=f"cost{t}", tag="cost")
             for h in range(2):
                 nc.vector.scalar_tensor_tensor(
-                    cost[t][:, cols[h]], logs[t][:, cols[h]], -1.0, cs_banks[t, h][:], ALU.mult, ALU.max
+                    cost[t][:, cols[h]], logs[t][:, cols[h]], -1.0, cs[t, h][:], ALU.mult, ALU.max
                 )
 
-        def add_transposed(dst, sources):
-            for n, src in enumerate(sources):
-                nc.tensor.matmul(dst, src, ident[:], start=(n == 0), stop=(n == len(sources) - 1), is_transpose=True)
+        def fetch_child(t, h, on_vector=False):
+            child[t, h] = work.tile([P, HALF], F32, name=f"child{t}{h}", tag="child", bufs=4)
+            picked = cost_window[t][:].indirect(chd_half[h])
+            if on_vector:
+                nc.vector.tensor_scalar(child[t, h][:], picked, 1.0 / COST_SHARE, 0.0, ALU.mult, ALU.add)
+            else:
+                nc.scalar.activation(child[t, h][:], picked, ACT.Copy, scale=1.0 / COST_SHARE)
 
-        def members(tile, h):
-            return [tile[:, HALF * h + d : HALF * (h + 1) : D] for d in range(D)]
-
-        def cost_sums(t, tag, bufs):
-            bank = psum.tile([P, V], F32, name=f"cost_bank{t}", tag=tag, bufs=bufs)
+        def join_choice(t):
             for h in range(2):
-                add_transposed(bank[:, P * h : P * (h + 1)], members(cost[t], h))
-            nc.scalar.activation(planes[t][:, V : 2 * V], bank[:], ACT.Copy, scale=0.64)
-
-        inp = {}
-        loop = {}
-        least = {}
-
-        def inputs(t, h):
-            inp[t, h] = work.tile([P, HALF], F32, name=f"inp{t}{h}", tag="inp", bufs=4)
-            nc.vector.tensor_tensor(inp[t, h][:], cost[t][:].indirect(chd_half[h]), sig[t][:, cols[h]], ALU.mult)
-
-        def inputs_split(t, h):
-            child = work.tile([P, HALF], F32, name=f"child{t}{h}", tag="child")
-            nc.scalar.activation(child[:], cost[t][:].indirect(chd_half[h]), ACT.Copy)
-            inp[t, h] = work.tile([P, HALF], F32, name=f"inp{t}{h}", tag="inp", bufs=4)
-            nc.vector.tensor_tensor(inp[t, h][:], child[:], sig[t][:, cols[h]], ALU.mult)
-
-        def loops(t, h):
-            loop[t, h] = work.tile([P, HALF], F32, name=f"loop{t}{h}", tag="loop")
-            nc.vector.tensor_tensor(loop[t, h][:], inp[t, h][:], factor[t, h][:], ALU.mult)
-
-        def lesser(t, h):
-            least[t, h] = work.tile([P, 2, 2 * P], F32, name=f"least{t}{h}", tag="least", bufs=4)
-            nc.vector.scalar_tensor_tensor(
-                least[t, h][:].rearrange("p e w -> p w e"),
-                cost[t][:, cols[h]].rearrange("p (w e) -> p w e", e=2),
-                0.36,
-                loop[t, h][:].rearrange("p (w e) -> p w e", e=2),
-                ALU.mult,
-                ALU.min,
-            )
-
-        def rest_sums(t, h, tag, bufs):
-            bank = psum.tile([P, P], F32, name=f"rest_bank{t}{h}", tag=tag, bufs=bufs)
-            add_transposed(bank[:], [inp[t, h][:, d::D] for d in range(D)] + [least[t, h][:, d % 2, d // 2 :: 2] for d in range(D)])
-            nc.scalar.copy(planes[t][:, 2 * V + P * h : 2 * V + P * (h + 1)], bank[:])
-
-        def join_choice(t, tags, split=()):
+                inp[t, h] = work.tile([P, HALF], F32, name=f"inp{t}{h}", tag="inp", bufs=4)
+                nc.vector.tensor_tensor(inp[t, h][:], child[t, h][:], sel[t][:, cols[h]], ALU.mult)
             for h in range(2):
-                (inputs_split if h in split else inputs)(t, h)
+                loop[t, h] = work.tile([P, HALF], F32, name=f"loop{t}{h}", tag="loop")
+                nc.vector.tensor_tensor(loop[t, h][:], inp[t, h][:], factor[t, h][:], ALU.mult)
             for h in range(2):
-                loops(t, h)
+                least[t, h] = work.tile([P, D, P], F32, name=f"least{t}{h}", tag="least", bufs=4)
+                nc.vector.scalar_tensor_tensor(
+                    least[t, h][:].rearrange("p d v -> p v d"),
+                    cost[t][:, cols[h]].rearrange("p (v d) -> p v d", d=D),
+                    0.36 / COST_SHARE,
+                    loop[t, h][:].rearrange("p (v d) -> p v d", d=D),
+                    ALU.mult,
+                    ALU.min,
+                )
+
+        def plan_sums(t):
             for h in range(2):
-                lesser(t, h)
-            for h in range(2):
-                rest_sums(t, h, *tags[h])
+                acc = bank_tile(cost_bank(t, h), P, f"sums{t}{h}")
+                terms = [cost[t][:, HALF * h + d : HALF * (h + 1) : D] for d in range(D)]
+                terms += [inp[t, h][:, d::D] for d in range(D)]
+                terms += [least[t, h][:, d, :] for d in range(D)]
+                for n, term in enumerate(terms):
+                    nc.tensor.matmul(
+                        acc[:], term, ident[:], start=(n == 0), stop=(n == len(terms) - 1), is_transpose=True
+                    )
+                nc.scalar.copy(planes[t][:, V + P * h : V + P * (h + 1)], acc[:])
 
         def plan_log(t):
-            plan_bank = psum.tile([P, HALF], F32, name=f"plan_bank{t}", tag="cs", bufs=4)
+            acc = bank_tile(cost_bank(t, 0), V, f"plan{t}")
             for h in range(2):
-                add_transposed(
-                    plan_bank[:, P * h : P * (h + 1)],
-                    [planes[t][:, V + P * h : V + P * (h + 1)], planes[t][:, 2 * V + P * h : 2 * V + P * (h + 1)]],
-                )
-            nc.scalar.activation(planes[t][:, :V], plan_bank[:, :V], ACT.Ln, bias=0.2)
+                nc.tensor.transpose(acc[:, P * h : P * (h + 1)], planes[t][:, V + P * h : V + P * (h + 1)], ident[:])
+            nc.scalar.activation(planes[t][:, :V], acc[:], ACT.Ln, bias=0.2, scale=COST_SHARE)
 
-        def weigh_frequencies(t):
-            nc.gpsimd.tensor_scalar(fq_unit[:, t, :], fq_sb[:, t, :], unit_sb[:, t : t + 1], 0.0, ALU.mult, ALU.add)
+        def slot_window(t, first, width):
+            return planes[t][:].indirect(wl_sb[:, first // 16 : (first + width) // 16])
 
-        def hidden_fused(t, pieces):
-            width = U // pieces
-            for n in range(pieces):
-                r = slice(width * n, width * (n + 1))
-                nc.vector.tensor_tensor(
-                    hid[:, t, r],
-                    planes[t][:].indirect(wl_sb[:, width // 16 * n : width // 16 * (n + 1)]),
-                    fq_unit[:, t, r],
-                    ALU.mult,
-                )
+        def fetch_logs(t, first, width):
+            slot_logs[t, first] = keep.tile([P, width], F32, name=f"slot_logs{t}_{first}")
+            nc.scalar.activation(slot_logs[t, first][:], slot_window(t, first, width), ACT.Copy)
 
-        fq_unit = keep.tile([P, PACK, U], F32, name="fq_unit")
-        slot_logs = {}
-
-        def fetch_logs(t, pieces):
-            width = U // pieces
-            for n in range(pieces):
-                slot_logs[t, n] = work.tile([P, width], F32, name=f"slot_logs{t}{n}", tag="slot_logs", bufs=3)
-                nc.scalar.activation(
-                    slot_logs[t, n][:], planes[t][:].indirect(wl_sb[:, width // 16 * n : width // 16 * (n + 1)]), ACT.Copy
-                )
-
-        def hidden(t, pieces):
-            width = U // pieces
-            for n in range(pieces):
-                r = slice(width * n, width * (n + 1))
-                nc.vector.scalar_tensor_tensor(
-                    hid[:, t, r], slot_logs[t, n][:], unit_sb[:, t : t + 1], fq_sb[:, t, r], ALU.mult, ALU.mult
-                )
-
-        cost_sigmoid(0)
-        cost_sigmoid(1)
-        selectivity(0)
-        quantise_tiles(w2_tiles, 1, 1)
-        round_half(w2_raw, w2_tiles, 0, nc.vector.tensor_copy, 2, 2)
-        round_half(w2_raw, w2_tiles, 1, nc.vector.tensor_copy, 2, 2)
-        quantise_tiles(w2_tiles, 2, 2)
-        quantise_tiles(w1_tiles, 2, 2)
-        for t in (3,):
-            weigh_frequencies(t)
-        child_factor(0, 0, True)
-        child_factor(0, 1, True)
-        for t in (0, 1):
-            cost_log(t)
-        finish_cost(0)
-        finish_cost(1)
-        selectivity(1, (("sum0", 1), ("sum1", 1)))
-        cost_sigmoid(2)
-        cost_sigmoid(3)
-        cost_sums(0, "se", 2)
-        cost_sums(1, "se", 2)
-        selectivity(2, (("sum0", 1), ("sum1", 1)))
-        selectivity(3)
-        child_factor(1, 1, False)
-        cost_log(2)
-        join_choice(0, [("sum0", 1), ("sum1", 1)])
-        cost_log(3)
-        child_factor(1, 0, True)
-        join_choice(1, [("se", 2), ("se", 2)])
-        finish_cost(2)
-        finish_cost(3)
-        child_factor(2, 0, False)
-        child_factor(2, 1, False)
-        cost_sums(2, "sum0", 1)
-        cost_sums(3, "sum1", 1)
-        plan_log(0)
-        child_factor(3, 0, False)
-        child_factor(3, 1, False)
-        plan_log(1)
-        join_choice(2, [("se", 2), ("se", 2)])
-        fetch_logs(0, 1)
-        fetch_logs(1, 1)
-        plan_log(2)
-        fetch_logs(2, 1)
-        join_choice(3, [("sum0", 1), ("sum1", 1)])
-        plan_log(3)
-        hidden(0, 1)
-        hidden(1, 1)
-        hidden(2, 1)
-
-        pieces = [(0, 128, nc.scalar.copy), (128, 128, nc.vector.tensor_copy), (256, 128, nc.scalar.copy), (384, 128, nc.vector.tensor_copy)]
-        last = PACK - 1
-        for first, width, copy in pieces:
+        def hidden(t, first, width):
             r = slice(first, first + width)
-            nc.vector.tensor_tensor(
-                hid[:, last, r],
-                planes[last][:].indirect(wl_sb[:, first // 16 : (first + width) // 16]),
-                fq_unit[:, last, r],
-                ALU.mult,
+            nc.vector.scalar_tensor_tensor(
+                hid[:, t, r], slot_logs[t, first][:], unit_sb[:, t : t + 1], fq_sb[:, t, r], ALU.mult, ALU.mult
             )
-        grouped = {}
-        for first, width, copy in pieces:
-            grouped[first] = keep.tile([P, width, PACK], BF16, name=f"hid_grouped{first}", align_bytes=64)
-            copy(grouped[first][:], hid[:, :, first : first + width].rearrange("p t r -> p r t"))
-        for first, width, copy in pieces:
-            codes = keep.tile([P, width], U32, name=f"hid_codes{first}", align_bytes=64)
-            scales = keep.tile([P, width], U8, name=f"hid_scales{first}", align_bytes=64)
+
+        last = PACK - 1
+        nc.gpsimd.tensor_scalar(fq_unit2[:], fq_sb[:, 2, V:], unit_sb[:, 2:3], 0.0, ALU.mult, ALU.add)
+        nc.gpsimd.tensor_scalar(
+            fq_unit[:, :V], fq_sb[:, last, :V], unit_sb[:, last : last + 1], 0.0, ALU.mult, ALU.add
+        )
+        for t in range(PACK):
+            selectivity(t)
+        for t in range(PACK):
+            cost_sigmoid(t)
+        for t in range(PACK):
+            for h in range(2):
+                if (t, h) != (last, 1):
+                    child_factor(t, h)
+        cost_log(0)
+        finish_cost(0)
+        cost_log(1)
+        finish_cost(1)
+        fetch_child(0, 0, True)
+        fetch_child(0, 1)
+        for t in range(PACK):
+            if t + 2 < PACK:
+                cost_log(t + 2)
+            if t + 1 < PACK:
+                fetch_child(t + 1, 0)
+                fetch_child(t + 1, 1)
+            if t + 1 == last:
+                child_factor(last, 1, False)
+            join_choice(t)
+            if t + 2 < PACK:
+                finish_cost(t + 2)
+            plan_sums(t)
+            plan_log(t)
+        for t in range(last):
+            for first in (0, V):
+                if (t, first) != (2, V):
+                    fetch_logs(t, first, V)
+        for t in range(last):
+            for first in (0, V):
+                if (t, first) != (2, V):
+                    hidden(t, first, V)
+        nc.vector.tensor_tensor(hid[:, 2, V:], slot_window(2, V, V), fq_unit2[:], ALU.mult)
+
+        for first in (2 * QUARTER, 3 * QUARTER):
+            fetch_logs(last, first, QUARTER)
+        for first in (0, QUARTER):
+            r = slice(first, first + QUARTER)
+            nc.vector.tensor_tensor(hid[:, last, r], slot_window(last, first, QUARTER), fq_unit[:, r], ALU.mult)
+        for first in (2 * QUARTER, 3 * QUARTER):
+            hidden(last, first, QUARTER)
+        grouped = []
+        for n in range(4):
+            grouped.append(keep.tile([P, QUARTER, PACK], BF16, name=f"hid_grouped{n}", align_bytes=64))
+            copy = nc.scalar.copy if n < 2 else nc.vector.tensor_copy
+            copy(grouped[n][:], hid[:, :, QUARTER * n : QUARTER * (n + 1)].rearrange("p t r -> p r t"))
+        for n in range(4):
+            codes = keep.tile([P, QUARTER], U32, name=f"hid_codes{n}", align_bytes=64)
+            scales = keep.tile([P, QUARTER], U8, name=f"hid_scales{n}", align_bytes=64)
             nc.vector.quantize_mx(
-                out=codes[:].bitcast(FP8X4), scales=scales[:], in_=grouped[first][:].rearrange("p r t -> p (r t)")
+                out=codes[:].bitcast(FP8X4), scales=scales[:], in_=grouped[n][:].rearrange("p r t -> p (r t)")
             )
-            bank = psum.tile([P, width], F32, name=f"out_bank{first}", tag="cs", bufs=4)
+            acc = bank_tile(4 + n, QUARTER, f"out{n}")
             nc.tensor.matmul_mx(
-                out=bank[:],
+                out=acc[:],
                 lhsT=w3_codes[:].bitcast(FP8X4),
                 lhsT_scale=w3_scales[:],
                 rhs=codes[:].bitcast(FP8X4),
@@ -356,6 +314,6 @@ def tile_picked_ydbtune_log_p_kernel(
                 start=True,
                 stop=True,
             )
-            result = keep.tile([P, width], F32, name=f"result{first}")
-            nc.scalar.copy(result[:], bank[:])
-            nc.sync.dma_start(out[:, first : first + width], result[:])
+            result = keep.tile([P, QUARTER], F32, name=f"result{n}")
+            nc.scalar.copy(result[:], acc[:])
+            (nc.sync if n % 2 == 0 else nc.scalar).dma_start(out[:, QUARTER * n : QUARTER * (n + 1)], result[:])

from contextlib import ExitStack

import concourse.mybir as mybir
from concourse.masks import make_identity

K, T, S, D, N, H, V, U = 512, 2048, 1024, 4, 128, 512, 256, 512
FLOPS = 2 * K * H * S * 2 + 2 * H * N * U

F32 = mybir.dt.float32
BF16 = mybir.dt.bfloat16
I32 = mybir.dt.int32
U32 = mybir.dt.uint32
U16 = mybir.dt.uint16
U8 = mybir.dt.uint8
FP8X4 = mybir.dt.float8_e4m3fn_x4
ACT = mybir.ActivationFunctionType
ALU = mybir.AluOpType

P = 128
PACK = 4
HALF = 512
QUARTER = 128
TINY = 2.0 ** -40
COST_SHARE = 0.64


def tile_picked_ydbtune_log_p_kernel(
    tc, x_words, x_scales, w1, w2, fq, unit, w3, offs, chd, wl, out
):
    nc = tc.nc
    with ExitStack() as ctx:
        keep = ctx.enter_context(tc.tile_pool(name="keep", bufs=1))
        work = ctx.enter_context(tc.tile_pool(name="work", bufs=2))
        psum = ctx.enter_context(tc.psum_pool(name="psum", bufs=1))

        offs_sb = keep.tile([P, S // 16], U16, name="offs_sb")
        chd_sb = keep.tile([P, S // 16], U16, name="chd_sb")
        wl_sb = keep.tile([P, U // 16], U16, name="wl_sb")
        x_table = keep.tile([P, T], I32, name="x_table")
        x_scale_table = keep.tile([P, T], U8, name="x_scale_table")
        sel = [keep.tile([P, 2 * S], F32, name=f"sel{t}") for t in range(PACK)]

        def load_weight_half(w, h, tile, queue):
            raw = tile[:, S:].rearrange("p (j c) -> p j c", j=PACK)
            queue.dma_start(raw, w.rearrange("(p j) c -> p j c", j=PACK)[:, :, h * 256 : (h + 1) * 256])
            return raw

        nc.vector.memset(x_scale_table[:].bitcast(I32), 0)
        w2_raw = [load_weight_half(w2, 0, sel[0], nc.scalar)]
        nc.sync.dma_start(offs_sb[:], offs)
        nc.sync.dma_start(chd_sb[:], chd)
        for quad in range(4):
            nc.sync.dma_start(
                x_scale_table[32 * quad : 32 * quad + 4, :].bitcast(I32),
                x_scales[0, 4 * quad : 4 * quad + 4, :].bitcast(I32),
            )
        nc.sync.dma_start(x_table[:], x_words[0].rearrange("p n t -> p (n t)").bitcast(I32))
        w2_raw.append(load_weight_half(w2, 1, sel[1], nc.sync))
        w1_raw = [load_weight_half(w1, h, sel[2 + h], nc.sync) for h in range(2)]
        w3_raw = keep.tile([P, PACK, N], F32, name="w3_raw")
        unit_sb = keep.tile([P, PACK], F32, name="unit_sb")
        fq_sb = keep.tile([P, PACK, U], F32, name="fq_sb")
        nc.sync.dma_start(w3_raw[:], w3.rearrange("(p j) c -> p j c", j=PACK))
        nc.sync.dma_start(unit_sb[:], unit.rearrange("(p t) o -> p (t o)", t=PACK))
        nc.sync.dma_start(fq_sb[:], fq.rearrange("(p t) r -> p t r", t=PACK))
        nc.sync.dma_start(wl_sb[:], wl)

        ident = keep.tile([P, P], F32, name="ident")
        make_identity(nc, ident[:])
        warm = keep.tile([P, 1], F32, name="warm")
        nc.scalar.activation(warm[:], ident[:, 0:1], ACT.Sigmoid)

        xg_words = [keep.tile([P, HALF], U32, name=f"xg_words{h}", align_bytes=64) for h in range(2)]
        xg_scales = [keep.tile([P, HALF], U8, name=f"xg_scales{h}", align_bytes=64) for h in range(2)]
        offs_half = [offs_sb[:, 32 * h : 32 * h + 32] for h in range(2)]
        chd_half = [chd_sb[:, 32 * h : 32 * h + 32] for h in range(2)]
        cols = [slice(HALF * h, HALF * (h + 1)) for h in range(2)]

        def weight_tiles(name):
            grouped = keep.tile([P, PACK, P, PACK], BF16, name=name + "_grouped", align_bytes=64)
            codes = keep.tile([P, H], U32, name=name + "_codes", align_bytes=64)
            scales = keep.tile([P, H], U8, name=name + "_scales", align_bytes=64)
            return grouped, codes, scales

        def round_part(raw, tiles, h, copy, first, count):
            copy(
                tiles[0][:, first : first + count, 64 * h : 64 * h + 64, :].rearrange("p t m j -> p m j t"),
                raw[h].rearrange("p j (m t) -> p m j t", t=PACK)[:, :, :, first : first + count],
            )

        def quantise_part(tiles, first, count):
            grouped, codes, scales = tiles
            nc.vector.quantize_mx(
                out=codes[:, P * first : P * (first + count)].bitcast(FP8X4),
                scales=scales[:, P * first : P * (first + count)],
                in_=grouped[:, first : first + count].rearrange("p t m j -> p (t m j)"),
            )

        w2_tiles = weight_tiles("w2")
        w1_tiles = weight_tiles("w1")
        for h in range(2):
            nc.vector.tensor_copy(xg_scales[h][:], x_scale_table[:].indirect(offs_half[h]))
        for h in range(2):
            nc.vector.tensor_copy(xg_words[h][:], x_table[:].bitcast(U32).indirect(offs_half[h]))
        round_part(w2_raw, w2_tiles, 0, nc.scalar.copy, 0, 4)
        round_part(w2_raw, w2_tiles, 1, nc.scalar.copy, 0, 2)
        quantise_part(w2_tiles, 0, 2)
        round_part(w2_raw, w2_tiles, 1, nc.scalar.copy, 2, 2)
        quantise_part(w2_tiles, 2, 2)
        round_part(w1_raw, w1_tiles, 0, nc.vector.tensor_copy, 0, 4)
        round_part(w1_raw, w1_tiles, 1, nc.vector.tensor_copy, 0, 4)
        quantise_part(w1_tiles, 0, 2)
        quantise_part(w1_tiles, 2, 2)

        w3_grouped = keep.tile([P, N, PACK], BF16, name="w3_grouped", align_bytes=64)
        w3_codes = keep.tile([P, N], U32, name="w3_codes", align_bytes=64)
        w3_scales = keep.tile([P, N], U8, name="w3_scales", align_bytes=64)
        nc.vector.tensor_copy(w3_grouped[:], w3_raw[:].rearrange("p j c -> p c j"))
        nc.vector.quantize_mx(
            out=w3_codes[:].bitcast(FP8X4), scales=w3_scales[:], in_=w3_grouped[:].rearrange("p c j -> p (c j)")
        )

        def bank_tile(bank, width, name):
            return psum.tile([P, width], F32, name=name, tag=f"bank{bank}")

        def product(tiles, t, h, bank, name):
            acc = bank_tile(bank, HALF, f"{name}{t}{h}")
            nc.tensor.matmul_mx(
                out=acc[:],
                lhsT=tiles[1][:, P * t : P * (t + 1)].bitcast(FP8X4),
                lhsT_scale=tiles[2][:, P * t : P * (t + 1)],
                rhs=xg_words[h][:].bitcast(FP8X4),
                rhs_scale=xg_scales[h][:],
                start=True,
                stop=True,
            )
            return acc

        def cost_bank(t, h):
            return (4 + 2 * t + h) % 8

        cs = {}
        cost_window = {}
        miss = {}
        logs = {}
        cost = {}
        factor = {}
        child = {}
        inp = {}
        loop = {}
        least = {}
        slot_logs = {}
        planes = [keep.tile([P, 2 * V], F32, name=f"plane{t}") for t in range(PACK)]
        hid = keep.tile([P, PACK, U], F32, name="hid")
        fq_unit2 = keep.tile([P, V], F32, name="fq_unit2")
        fq_unit = keep.tile([P, V], F32, name="fq_unit")

        def selectivity(t):
            for h in range(2):
                acc = product(w2_tiles, t, h, (2 * t + h) % 4, "se")
                nc.scalar.activation(sel[t][:, cols[h]], acc[:], ACT.Sigmoid)

        def cost_sigmoid(t):
            cost_window[t] = keep.tile([P, 2 * S], F32, name=f"cost{t}")
            cost[t] = cost_window[t][:, :S]
            miss[t] = cost_window[t][:, S:]
            for h in range(2):
                cs[t, h] = product(w1_tiles, t, h, cost_bank(t, h), "cs")
                nc.scalar.activation(miss[t][:, cols[h]], cs[t, h][:], ACT.Sigmoid, scale=-1.0)

        def cost_log(t):
            logs[t] = work.tile([P, S], F32, name=f"logs{t}", tag="logs")
            for h in range(2):
                nc.scalar.activation(logs[t][:, cols[h]], miss[t][:, cols[h]], ACT.Ln, bias=TINY)

        def child_factor(t, h, on_vector=True):
            factor[t, h] = keep.tile([P, HALF], F32, name=f"factor{t}{h}")
            picked = sel[t][:].indirect(chd_half[h])
            if on_vector:
                nc.vector.tensor_scalar(factor[t, h][:], picked, 1.6, -0.52, ALU.mult, ALU.add)
            else:
                nc.scalar.activation(factor[t, h][:], picked, ACT.Copy, bias=-0.52, scale=1.6)

        def finish_cost(t):
            for h in range(2):
                nc.vector.scalar_tensor_tensor(
                    cost[t][:, cols[h]], logs[t][:, cols[h]], -1.0, cs[t, h][:], ALU.mult, ALU.max
                )

        def fetch_child(t, h, on_vector=False):
            child[t, h] = work.tile([P, HALF], F32, name=f"child{t}{h}", tag="child", bufs=4)
            picked = cost_window[t][:].indirect(chd_half[h])
            if on_vector:
                nc.vector.tensor_scalar(child[t, h][:], picked, 1.0 / COST_SHARE, 0.0, ALU.mult, ALU.add)
            else:
                nc.scalar.activation(child[t, h][:], picked, ACT.Copy, scale=1.0 / COST_SHARE)

        def join_choice(t):
            for h in range(2):
                inp[t, h] = work.tile([P, HALF], F32, name=f"inp{t}{h}", tag="inp", bufs=4)
                nc.vector.tensor_tensor(inp[t, h][:], child[t, h][:], sel[t][:, cols[h]], ALU.mult)
            for h in range(2):
                loop[t, h] = work.tile([P, HALF], F32, name=f"loop{t}{h}", tag="loop")
                nc.vector.tensor_tensor(loop[t, h][:], inp[t, h][:], factor[t, h][:], ALU.mult)
            for h in range(2):
                least[t, h] = work.tile([P, D, P], F32, name=f"least{t}{h}", tag="least", bufs=4)
                nc.vector.scalar_tensor_tensor(
                    least[t, h][:].rearrange("p d v -> p v d"),
                    cost[t][:, cols[h]].rearrange("p (v d) -> p v d", d=D),
                    0.36 / COST_SHARE,
                    loop[t, h][:].rearrange("p (v d) -> p v d", d=D),
                    ALU.mult,
                    ALU.min,
                )

        def plan_sums(t):
            for h in range(2):
                acc = bank_tile(cost_bank(t, h), P, f"sums{t}{h}")
                terms = [cost[t][:, HALF * h + d : HALF * (h + 1) : D] for d in range(D)]
                terms += [inp[t, h][:, d::D] for d in range(D)]
                terms += [least[t, h][:, d, :] for d in range(D)]
                for n, term in enumerate(terms):
                    nc.tensor.matmul(
                        acc[:], term, ident[:], start=(n == 0), stop=(n == len(terms) - 1), is_transpose=True
                    )
                nc.scalar.copy(planes[t][:, V + P * h : V + P * (h + 1)], acc[:])

        def plan_log(t):
            acc = bank_tile(cost_bank(t, 0), V, f"plan{t}")
            for h in range(2):
                nc.tensor.transpose(acc[:, P * h : P * (h + 1)], planes[t][:, V + P * h : V + P * (h + 1)], ident[:])
            nc.scalar.activation(planes[t][:, :V], acc[:], ACT.Ln, bias=0.2, scale=COST_SHARE)

        def slot_window(t, first, width):
            return planes[t][:].indirect(wl_sb[:, first // 16 : (first + width) // 16])

        def fetch_logs(t, first, width):
            slot_logs[t, first] = keep.tile([P, width], F32, name=f"slot_logs{t}_{first}")
            nc.scalar.activation(slot_logs[t, first][:], slot_window(t, first, width), ACT.Copy)

        def hidden(t, first, width):
            r = slice(first, first + width)
            nc.vector.scalar_tensor_tensor(
                hid[:, t, r], slot_logs[t, first][:], unit_sb[:, t : t + 1], fq_sb[:, t, r], ALU.mult, ALU.mult
            )

        last = PACK - 1
        nc.gpsimd.tensor_scalar(fq_unit2[:], fq_sb[:, 2, V:], unit_sb[:, 2:3], 0.0, ALU.mult, ALU.add)
        nc.gpsimd.tensor_scalar(
            fq_unit[:, :V], fq_sb[:, last, :V], unit_sb[:, last : last + 1], 0.0, ALU.mult, ALU.add
        )
        for t in range(PACK):
            selectivity(t)
        for t in range(PACK):
            cost_sigmoid(t)
        for t in range(PACK):
            for h in range(2):
                if (t, h) != (last, 1):
                    child_factor(t, h)
        cost_log(0)
        finish_cost(0)
        cost_log(1)
        finish_cost(1)
        fetch_child(0, 0, True)
        fetch_child(0, 1)
        for t in range(PACK):
            if t + 2 < PACK:
                cost_log(t + 2)
            if t + 1 < PACK:
                fetch_child(t + 1, 0)
                fetch_child(t + 1, 1)
            if t + 1 == last:
                child_factor(last, 1, False)
            join_choice(t)
            if t + 2 < PACK:
                finish_cost(t + 2)
            plan_sums(t)
            plan_log(t)
        for t in range(last):
            for first in (0, V):
                if (t, first) != (2, V):
                    fetch_logs(t, first, V)
        for t in range(last):
            for first in (0, V):
                if (t, first) != (2, V):
                    hidden(t, first, V)
        nc.vector.tensor_tensor(hid[:, 2, V:], slot_window(2, V, V), fq_unit2[:], ALU.mult)

        for first in (2 * QUARTER, 3 * QUARTER):
            fetch_logs(last, first, QUARTER)
        for first in (0, QUARTER):
            r = slice(first, first + QUARTER)
            nc.vector.tensor_tensor(hid[:, last, r], slot_window(last, first, QUARTER), fq_unit[:, r], ALU.mult)
        for first in (2 * QUARTER, 3 * QUARTER):
            hidden(last, first, QUARTER)
        grouped = []
        for n in range(4):
            grouped.append(keep.tile([P, QUARTER, PACK], BF16, name=f"hid_grouped{n}", align_bytes=64))
            copy = nc.scalar.copy if n < 2 else nc.vector.tensor_copy
            copy(grouped[n][:], hid[:, :, QUARTER * n : QUARTER * (n + 1)].rearrange("p t r -> p r t"))
        for n in range(4):
            codes = keep.tile([P, QUARTER], U32, name=f"hid_codes{n}", align_bytes=64)
            scales = keep.tile([P, QUARTER], U8, name=f"hid_scales{n}", align_bytes=64)
            nc.vector.quantize_mx(
                out=codes[:].bitcast(FP8X4), scales=scales[:], in_=grouped[n][:].rearrange("p r t -> p (r t)")
            )
            acc = bank_tile(4 + n, QUARTER, f"out{n}")
            nc.tensor.matmul_mx(
                out=acc[:],
                lhsT=w3_codes[:].bitcast(FP8X4),
                lhsT_scale=w3_scales[:],
                rhs=codes[:].bitcast(FP8X4),
                rhs_scale=scales[:],
                start=True,
                stop=True,
            )
            result = keep.tile([P, QUARTER], F32, name=f"result{n}")
            nc.scalar.copy(result[:], acc[:])
            (nc.sync if n % 2 == 0 else nc.scalar).dma_start(out[:, QUARTER * n : QUARTER * (n + 1)], result[:])
